import numpy as np
import ml_dtypes


def mxq(x, axis, fmt="e4m3"):
    dtype, down = {"e4m3": (ml_dtypes.float8_e4m3fn, 7), "e5m2": (ml_dtypes.float8_e5m2, 14)}[fmt]
    v = np.moveaxis(np.asarray(x, np.float32).astype(ml_dtypes.bfloat16).astype(np.float64), axis, -1)
    blocks = v.reshape(v.shape[:-1] + (-1, 32))
    amax = np.abs(blocks).max(-1, keepdims=True)
    byte = np.maximum(np.where(amax > 0, np.frexp(amax)[1] - 1 + 127, 0) - down, 1)
    scale = np.exp2(byte - 127.0)
    codes = (blocks / scale).astype(np.float32).astype(dtype).astype(np.float64)
    return np.moveaxis((codes * scale).reshape(v.shape), -1, axis)


WIDE = False


def mx_kscale(k):
    if not WIDE:
        return np.ones(k)
    levels = np.array([10, -10, 5, -5, 0])
    if k % 512:
        return np.exp2(np.random.permutation(np.resize(levels, k // 32))).repeat(32)
    a = np.empty((k // 512, 16))
    for p in range(k // 512):
        a[p, :8] = np.random.permutation(np.resize(levels, 8))
        for g in range(8):
            far = levels[np.abs(levels - a[p, g]) >= 10]
            a[p, g + 8] = far[np.random.randint(len(far))]
    return np.exp2(a.ravel()).repeat(32)


def f64(x):
    return np.asarray(x).astype(np.float64)


def striped(idx):
    return np.tile(np.asarray(idx).reshape(-1, 16).T, (8, 1)).astype(np.uint16)


def unstriped(offs):
    return offs[:16].T.reshape(-1).astype(np.int64)


E2M1 = np.array([0.0, 0.5, 1.0, 1.5, 2.0, 3.0, 4.0, 6.0, -0.0, -0.5, -1.0, -1.5, -2.0, -3.0, -4.0, -6.0])


def pack_weight(w, fmt):
    k, n = w.shape
    w = f64(np.asarray(w, np.float32).astype(ml_dtypes.bfloat16)).reshape(k // 32, 32, n)
    amax = np.abs(w).max(1)
    if fmt == "e4m3":
        byte = np.frexp(amax)[1] - 1 + 127 - 7
    else:
        mant, ex = np.frexp(amax / 6.0)
        byte = np.where(mant > 0.5, ex, ex - 1) + 127
    byte = np.clip(np.where(amax > 0, byte, 1), 1, 254)
    scaled = (w * np.exp2(127.0 - byte)[:, None, :]).reshape(k, n).astype(np.float32)
    by_word = np.ascontiguousarray(scaled.reshape(k // 512, 128, 4, n).transpose(0, 1, 3, 2))
    if fmt == "e4m3":
        words = by_word.astype(ml_dtypes.float8_e4m3fn).view(np.uint8)
    else:
        c = by_word.astype(ml_dtypes.float4_e2m1fn).view(np.uint8) & 0xF
        words = (c[..., 0::2] | (c[..., 1::2] << 4)).reshape(k // 512, 128, 2 * n)
    return np.ascontiguousarray(words), np.ascontiguousarray(byte.astype(np.uint8).reshape(k // 512, 16, n))


def unpack_weight(words, scales, fmt):
    g, _, n = scales.shape
    words = np.ascontiguousarray(words).reshape(g, 128, n, -1)
    if fmt == "e4m3":
        vals = words.view(ml_dtypes.float8_e4m3fn).astype(np.float64)
    else:
        nib = np.empty((g, 128, n, 4), np.uint8)
        nib[..., 0::2] = words & 0xF
        nib[..., 1::2] = words >> 4
        vals = E2M1[nib]
    vals = vals * np.repeat(np.exp2(scales.astype(np.float64) - 127.0), 8, axis=1)[..., None]
    return vals.transpose(0, 1, 3, 2).reshape(g * 512, n)


D, E, T, I, Q = 512, 512, 2048, 512, 128


def setup_inputs():
    n = np.random.standard_normal
    idx = np.random.permutation(T)[:I]
    fd = mx_kscale(D)
    fe = mx_kscale(E)
    keysp = pack_weight(n((D, T)) / fd[:, None], "e2m1")
    valsp = pack_weight(n((E, T)) / fe[:, None], "e2m1")
    return {
        "query": (n((D, Q)) * 0.8 / np.sqrt(D) * fd[:, None]).astype(np.float32),
        "keys_words": keysp[0],
        "keys_scales": keysp[1],
        "damp": (np.random.uniform(1.0, 4.0, (Q, 1))).astype(np.float32),
        "gout": (n((E, Q)) * 1 / np.sqrt(E) * fe[:, None]).astype(np.float32),
        "vals_words": valsp[0],
        "vals_scales": valsp[1],
        "base": (0.5 * n((Q, I))).astype(np.float32),
        "offs": striped(idx),
    }


def reference(query, keys_words, keys_scales, damp, gout, vals_words, vals_scales, base, offs):
    idx = unstriped(offs)
    keysu = unpack_weight(keys_words, keys_scales, "e2m1")
    valsu = unpack_weight(vals_words, vals_scales, "e2m1")
    queryq = mxq(f64(query), 0, "e4m3")
    keysidxg = keysu[:, idx]
    a = queryq.T @ keysidxg
    p = np.exp(a - np.max(a, axis=1, keepdims=True))
    r = p / np.sum(p, axis=1, keepdims=True) * 512.0
    u0 = np.log(r * f64(damp) + 1.0)
    goutq = mxq(f64(gout), 0, "e4m3")
    valsidxg = valsu[:, idx]
    c0 = goutq.T @ valsidxg
    du0 = c0 / np.sum(u0, axis=1, keepdims=True) + np.sum(c0 * u0 / np.square(np.sum(u0, axis=1, keepdims=True)) * (-1.0), axis=1, keepdims=True)
    dr = du0 / (r * f64(damp) + 1.0) * f64(damp)
    dp = dr * 512.0 / np.sum(p, axis=1, keepdims=True) + np.sum(dr * 512.0 * p / np.square(np.sum(p, axis=1, keepdims=True)) * (-1.0), axis=1, keepdims=True)
    da = dp * p
    hda = da * 512.0 * 2.0 * 512.0
    hdp = hda * p
    hdr = hdp / np.sum(p, axis=1, keepdims=True) * 512.0 + np.sum(hdp, axis=1, keepdims=True) * (-1.0) / np.square(np.sum(p, axis=1, keepdims=True)) * p * 512.0
    hdu0 = hdr * f64(damp) / (r * f64(damp) + 1.0)
    hu0 = np.sum(hdu0 * c0 / np.square(np.sum(u0, axis=1, keepdims=True)) * (-1.0), axis=1, keepdims=True) + np.sum(hdu0, axis=1, keepdims=True) * (-1.0) / np.square(np.sum(u0, axis=1, keepdims=True)) * c0 + np.sum(np.sum(hdu0, axis=1, keepdims=True) * (-1.0) * c0 * u0 / np.square(np.square(np.sum(u0, axis=1, keepdims=True))) * (-1.0), axis=1, keepdims=True) * np.sum(u0, axis=1, keepdims=True) * 2.0
    hr = hdr * f64(damp) * du0 / np.square(r * f64(damp) + 1.0) * (-1.0) * f64(damp) + hu0 / (r * f64(damp) + 1.0) * f64(damp)
    hp = hda * dp + np.sum(hdp * dr * 512.0 / np.square(np.sum(p, axis=1, keepdims=True)) * (-1.0), axis=1, keepdims=True) + np.sum(hdp, axis=1, keepdims=True) * (-1.0) / np.square(np.sum(p, axis=1, keepdims=True)) * dr * 512.0 + np.sum(np.sum(hdp, axis=1, keepdims=True) * (-1.0) * dr * 512.0 * p / np.square(np.square(np.sum(p, axis=1, keepdims=True))) * (-1.0), axis=1, keepdims=True) * np.sum(p, axis=1, keepdims=True) * 2.0 + hr * 512.0 / np.sum(p, axis=1, keepdims=True) + np.sum(hr * 512.0 * p / np.square(np.sum(p, axis=1, keepdims=True)) * (-1.0), axis=1, keepdims=True)
    ha = hp * p
    y = ha + f64(base)
    return y

@@ -1,0 +1,225 @@
+import math
+from contextlib import ExitStack
+
+import concourse.mybir as mybir
+
+F32 = mybir.dt.float32
+BF16 = mybir.dt.bfloat16
+I32 = mybir.dt.int32
+U32 = mybir.dt.uint32
+U16 = mybir.dt.uint16
+U8 = mybir.dt.uint8
+FP8X4 = mybir.dt.float8_e4m3fn_x4
+FP4X4 = mybir.dt.float4_e2m1fn_x4
+ALU = mybir.AluOpType
+ACT = mybir.ActivationFunctionType
+
+P = 128
+PACK = 4
+TOKENS = 2048
+SLOTS = 512
+HALF = SLOTS // 2
+HALVES = [slice(0, HALF), slice(HALF, SLOTS)]
+ROOT_K = math.sqrt(2.0 * SLOTS * SLOTS)
+FLOPS = 2 * 2 * 512 * 128 * 512
+
+
+def tile_attend_gpdirect_dampened_kernel(tc, query, keys_words, keys_scales, damp, gout, vals_words, vals_scales, base, offs, out):
+    nc = tc.nc
+    with ExitStack() as ctx:
+        sb = ctx.enter_context(tc.tile_pool(name="sb", bufs=1))
+        ps = ctx.enter_context(tc.psum_pool(name="ps", bufs=1))
+
+        def wide(name, width=SLOTS):
+            return sb.tile([P, width], F32, name=name, align_bytes=64)
+
+        def col(name, width=1):
+            return sb.tile([P, width], F32, name=name)
+
+        def fma(name, x, scale, bias):
+            r = col(name, x.shape[1])
+            nc.scalar.activation(r[:], x, ACT.Identity, bias=bias, scale=scale)
+            return r
+
+        def fma_sum(name, x, scale, bias):
+            terms = col(name + "_terms", 2)
+            r = col(name)
+            nc.scalar.activation(terms[:], x[:], ACT.Identity, bias=bias, scale=scale, accum_out=r[:])
+            return r
+
+        def mul2(dst, x, s1, s2):
+            nc.gpsimd.tensor_scalar(dst, x, s1, s2, ALU.mult, ALU.mult)
+
+        offsets = sb.tile([P, SLOTS // 16], U16, name="offsets")
+        k_words = sb.tile([P, TOKENS], U16, name="k_words", align_bytes=64)
+        v_words = sb.tile([P, TOKENS], U16, name="v_words", align_bytes=64)
+        k_bytes = sb.tile([P, TOKENS], U8, name="k_bytes", align_bytes=64)
+        v_bytes = sb.tile([P, TOKENS], U8, name="v_bytes", align_bytes=64)
+        q_raw = sb.tile([P, PACK, P], F32, name="q_raw", tag="stage", align_bytes=64)
+        damp_sb = sb.tile([P, 1], F32, name="damp_sb", tag="early", align_bytes=64)
+
+        nc.vector.memset(k_bytes[:].bitcast(I32), 0)
+        nc.gpsimd.memset(v_bytes[:].bitcast(I32), 0)
+
+        nc.sync.dma_start(offsets[:], offs)
+        nc.sync.dma_start(k_words[:].bitcast(I32), keys_words[0].bitcast(I32))
+        nc.sync.dma_start(q_raw[:], query.rearrange("(p j) q -> p j q", j=PACK))
+        nc.sync.dma_start(damp_sb[:], damp)
+        for quad in range(4):
+            nc.sync.dma_start(k_bytes[32 * quad : 32 * quad + 4, :].bitcast(I32), keys_scales[0, 4 * quad : 4 * quad + 4, :].bitcast(I32))
+        g_raw = sb.tile([P, PACK, P], F32, name="g_raw", align_bytes=64)
+        nc.gpsimd.dma_start(g_raw[:], gout.rearrange("(p j) q -> p j q", j=PACK))
+        nc.gpsimd.dma_start(v_words[:].bitcast(I32), vals_words[0].bitcast(I32))
+        for quad in range(4):
+            nc.sync.dma_start(v_bytes[32 * quad : 32 * quad + 4, :].bitcast(I32), vals_scales[0, 4 * quad : 4 * quad + 4, :].bitcast(I32))
+
+        def quantise(name, grouped, tag):
+            codes = sb.tile([P, P], U32, name=name + "_codes", align_bytes=64)
+            scales = sb.tile([P, P], U8, name=name + "_scales", tag=tag, align_bytes=64)
+            nc.vector.quantize_mx(out=codes[:].bitcast(FP8X4), scales=scales[:], in_=grouped[:].rearrange("p q j -> p (q j)"))
+            return codes, scales
+
+        def gather(picked, window, lst):
+            nc.vector.tensor_copy(picked, window[:].indirect(lst))
+
+        def product(name, stationary, words, scale_bytes):
+            bank = ps.tile([P, HALF], F32, name=name)
+            nc.tensor.matmul_mx(out=bank[:], lhsT=stationary[0][:].bitcast(FP8X4), lhsT_scale=stationary[1][:],
+                                rhs=words.bitcast(FP4X4), rhs_scale=scale_bytes, start=True, stop=True)
+            return bank
+
+        lists = [offsets[:, 0:16], offsets[:, 16:32]]
+
+        q_bf = sb.tile([P, P, PACK], BF16, name="q_bf", align_bytes=64)
+        nc.scalar.activation(q_bf[:], q_raw[:].rearrange("p j q -> p q j"), ACT.Copy)
+        g_bf = sb.tile([P, P, PACK], BF16, name="g_bf", align_bytes=64)
+        nc.scalar.activation(g_bf[:], g_raw[:].rearrange("p j q -> p q j"), ACT.Copy)
+        base_sb = sb.tile([P, SLOTS], F32, name="base_sb", tag="stage", align_bytes=64)
+        nc.sync.dma_start(base_sb[:], base)
+
+        kw = sb.tile([P, SLOTS], U16, name="kw", align_bytes=64)
+        gather(kw[:], k_words, offsets[:])
+        q_mx = quantise("q", q_bf, "q_scales")
+        a = []
+        for i, cols in enumerate(HALVES):
+            kb = sb.tile([P, HALF], U8, name=f"kb{i}", tag=f"kb{i}", align_bytes=64)
+            gather(kb[:], k_bytes, lists[i])
+            a.append(product(f"a{i}", q_mx, kw[:, cols], kb[:]))
+
+        nm0 = col("nm0")
+        nc.vector.tensor_reduce(nm0[:], a[0][:], mybir.AxisListType.X, ALU.max, negate=True)
+        nm = col("nm")
+        neg_a1 = wide("neg_a1", HALF)
+        nc.vector.tensor_scalar(neg_a1[:], a[1][:], -1.0, nm0[:], ALU.mult, ALU.min, accum_out=nm[:])
+        p = wide("p")
+        p0 = wide("p0", HALF)
+        s0 = col("s0")
+        s1 = col("s1")
+        nc.scalar.activation(p0[:], a[0][:], ACT.Exp, bias=nm0[:], scale=1.0, accum_out=s0[:])
+        nc.scalar.activation(p[:, HALVES[1]], neg_a1[:], ACT.Exp, bias=nm[:], scale=-1.0, accum_out=s1[:])
+        f0 = col("f0")
+        nc.scalar.activation(f0[:], nm0[:], ACT.Exp, bias=nm[:], scale=-1.0)
+
+        und = col("und", 2)
+        mul2(und[:, 1:2], damp_sb[:], float(SLOTS), 1.0)
+        vw = sb.tile([P, SLOTS], U16, name="vw", align_bytes=64)
+        gather(vw[:], v_words, offsets[:])
+        s = col("s")
+        nc.vector.tensor_scalar(s[:], s0[:], f0[:], s1[:], ALU.mult, ALU.add)
+        nc.vector.tensor_scalar(p[:, HALVES[0]], p0[:], f0[:], None, ALU.mult)
+        rs = col("rs")
+        nc.vector.reciprocal(rs[:], s[:])
+        g_mx = quantise("g", g_bf, "kb1")
+        kappa = col("kappa")
+        nc.vector.tensor_scalar(kappa[:], rs[:], damp_sb[:], float(SLOTS), ALU.mult, ALU.mult)
+        vb = sb.tile([P, SLOTS], U8, name="vb", tag="early", align_bytes=64)
+        c = []
+        for i, cols in enumerate(HALVES):
+            gather(vb[:, cols], v_bytes, lists[i])
+            c.append(product(f"c{i}", g_mx, vw[:, cols], vb[:, cols]))
+
+        u = wide("u")
+        nc.scalar.activation(u[:], p[:], ACT.Ln, bias=1.0, scale=kappa[:], accum_out=und[:, 0:1])
+        qq = wide("qq")
+        qs = col("qs", 2)
+        for i, cols in enumerate(HALVES):
+            nc.scalar.activation(qq[:, cols], u[:, cols], ACT.Exp, scale=-1.0, accum_out=qs[:, i : i + 1])
+
+        nrs = col("nrs")
+        mul2(nrs[:], rs[:], -1.0, 1.0)
+        nrs2 = col("nrs2")
+        mul2(nrs2[:], rs[:], rs[:], -1.0)
+        rsnh = col("rsnh")
+        mul2(rsnh[:], rs[:], float(HALF), 1.0)
+        ct = col("ct", 2)
+        mul2(ct[:, 1:2], rs[:], 0.5, 1.0)
+
+        r2 = col("r2", 2)
+        nc.vector.reciprocal(r2[:], und[:])
+        ru = r2[:, 0:1]
+        idl = r2[:, 1:2]
+        ks = col("ks")
+        mul2(ks[:], kappa[:], ru, ROOT_K)
+        rsigh = col("rsigh")
+        mul2(rsigh[:], rs[:], ru, 0.5 * ROOT_K)
+        nr2 = col("nr2", 2)
+        mul2(nr2[:], r2[:], -1.0, 1.0)
+        nru = nr2[:, 0:1]
+        nidl = nr2[:, 1:2]
+        mul2(ct[:, 0:1], ru, -0.5, 1.0)
+        ruidlh = col("ruidlh")
+        mul2(ruidlh[:], ru, idl, 0.5)
+
+        uc_terms = wide("uc_terms")
+        uc = col("uc", 2)
+        for i, cols in enumerate(HALVES):
+            nc.vector.scalar_tensor_tensor(uc_terms[:, cols], c[i][:], 1.0, u[:, cols], ALU.mult, ALU.mult, accum_out=uc[:, i : i + 1])
+        f = col("f")
+        nc.vector.tensor_scalar(f[:], uc[:, 0:1], uc[:, 1:2], ru, ALU.add, ALU.mult)
+        dp = wide("dp")
+        pd = col("pd", 2)
+        for i, cols in enumerate(HALVES):
+            nc.vector.scalar_tensor_tensor(dp[:, cols], c[i][:], f[:], p[:, cols], ALU.subtract, ALU.mult, accum_out=pd[:, i : i + 1])
+
+        def halves(name, in0, scalar, in1, op0, op1, with_sum):
+            r = wide(name)
+            sums = col(name + "_sums", 2) if with_sum else None
+            for i, cols in enumerate(HALVES):
+                nc.vector.scalar_tensor_tensor(r[:, cols], in0[:, cols], scalar, in1[:, cols], op0, op1,
+                                               accum_out=sums[:, i : i + 1] if with_sum else None)
+            return r, sums
+
+        h, hs = halves("h", dp, ks[:], qq, ALU.mult, ALU.mult, True)
+        nht, nth = halves("nht", qq, 1.0, h, ALU.subtract, ALU.mult, True)
+
+        p_sq = wide("p_sq")
+        p2 = col("p2")
+        nc.scalar.activation(p_sq[:], p[:], ACT.Square, accum_out=p2[:])
+        na = fma_sum("na", hs, nrs[:], 0.0)
+        e = fma("e", p2[:], nrs2[:], nidl)
+        tt = fma_sum("tt", qs, -1.0, float(HALF))
+        b0h = fma_sum("b0h", pd, rsigh[:], 0.0)
+        cth = fma("cth", tt[:], ruidlh[:], ct[:, 0:1])
+        beta = fma_sum("beta", hs, e[:], b0h[:])
+        tv = fma("tv", ct[:], tt[:], 0.0)
+        y1h = fma_sum("y1h", hs, cth[:], 0.0)
+        y2h = fma("y2h", beta[:], tv[:, 0:1], y1h[:])
+        aa = fma_sum("aa", nth, nru, y2h[:])
+
+        g = halves("g", p, na[:], h, ALU.mult, ALU.add, False)[0]
+        g_sq = wide("g_sq")
+        bs = col("bs")
+        nc.scalar.activation(g_sq[:], g[:], ACT.Square, accum_out=bs[:])
+        ab = fma("ab", aa[:], beta[:], 0.0)
+        b = fma("b", bs[:], ru, 0.0)
+        e4 = fma("e4", ab[:], rsnh[:], 0.0)
+        cb = fma("cb", bs[:], ru, ab[:])
+        e3h = fma("e3h", b[:], tv[:, 1:2], e4[:])
+        m = halves("m", g, aa[:], nht, ALU.subtract, ALU.add, False)[0]
+        x, xs = halves("x", g, beta[:], m, ALU.subtract, ALU.mult, True)
+        ng = fma_sum("ng", xs, nrs[:], e3h[:])
+        r = halves("r", qq, b[:], base_sb, ALU.mult, ALU.add, False)[0]
+        z = halves("z", x, cb[:], r, ALU.subtract, ALU.add, False)[0]
+        y = halves("y", p, ng[:], z, ALU.mult, ALU.add, False)[0]
+        nc.sync.dma_start(out[:, HALVES[0]], y[:, HALVES[0]])
+        nc.scalar.dma_start(out[:, HALVES[1]], y[:, HALVES[1]])

@@ -47,31 +47,32 @@ def tile_attend_gpdirect_dampened_kernel(tc, query, keys_words, keys_scales, dam
             nc.scalar.activation(terms[:], x[:], ACT.Identity, bias=bias, scale=scale, accum_out=r[:])
             return r
 
-        def mul2(dst, x, s1, s2):
-            nc.gpsimd.tensor_scalar(dst, x, s1, s2, ALU.mult, ALU.mult)
-
         offsets = sb.tile([P, SLOTS // 16], U16, name="offsets")
         k_words = sb.tile([P, TOKENS], U16, name="k_words", align_bytes=64)
         v_words = sb.tile([P, TOKENS], U16, name="v_words", align_bytes=64)
-        k_bytes = sb.tile([P, TOKENS], U8, name="k_bytes", align_bytes=64)
+        k_bytes = sb.tile([P, TOKENS], U8, name="k_bytes", tag="k_bytes", align_bytes=64)
         v_bytes = sb.tile([P, TOKENS], U8, name="v_bytes", align_bytes=64)
-        q_raw = sb.tile([P, PACK, P], F32, name="q_raw", tag="stage", align_bytes=64)
-        damp_sb = sb.tile([P, 1], F32, name="damp_sb", tag="early", align_bytes=64)
+        q_raw = sb.tile([P, PACK, P], F32, name="q_raw", tag="q_raw", align_bytes=64)
+        g_raw = sb.tile([P, PACK, P], F32, name="g_raw", tag="g_raw", align_bytes=64)
+        damp_sb = col("damp_sb")
+        base_sb = wide("base_sb")
 
         nc.vector.memset(k_bytes[:].bitcast(I32), 0)
-        nc.gpsimd.memset(v_bytes[:].bitcast(I32), 0)
+        nc.vector.memset(v_bytes[:].bitcast(I32), 0)
 
-        nc.sync.dma_start(offsets[:], offs)
-        nc.sync.dma_start(k_words[:].bitcast(I32), keys_words[0].bitcast(I32))
+        def load_scales(plane, rows, queues):
+            for quad, queue in enumerate(queues):
+                queue.dma_start(plane[32 * quad : 32 * quad + 4, :].bitcast(I32), rows[0, 4 * quad : 4 * quad + 4, :].bitcast(I32))
+
         nc.sync.dma_start(q_raw[:], query.rearrange("(p j) q -> p j q", j=PACK))
-        nc.sync.dma_start(damp_sb[:], damp)
-        for quad in range(4):
-            nc.sync.dma_start(k_bytes[32 * quad : 32 * quad + 4, :].bitcast(I32), keys_scales[0, 4 * quad : 4 * quad + 4, :].bitcast(I32))
-        g_raw = sb.tile([P, PACK, P], F32, name="g_raw", align_bytes=64)
-        nc.gpsimd.dma_start(g_raw[:], gout.rearrange("(p j) q -> p j q", j=PACK))
-        nc.gpsimd.dma_start(v_words[:].bitcast(I32), vals_words[0].bitcast(I32))
-        for quad in range(4):
-            nc.sync.dma_start(v_bytes[32 * quad : 32 * quad + 4, :].bitcast(I32), vals_scales[0, 4 * quad : 4 * quad + 4, :].bitcast(I32))
+        nc.scalar.dma_start(damp_sb[:], damp)
+        nc.sync.dma_start(offsets[:], offs)
+        load_scales(k_bytes, keys_scales, (nc.sync,) * 4)
+        nc.sync.dma_start(k_words[:].bitcast(I32), keys_words[0].bitcast(I32))
+        nc.sync.dma_start(g_raw[:], gout.rearrange("(p j) q -> p j q", j=PACK))
+        nc.sync.dma_start(v_words[:].bitcast(I32), vals_words[0].bitcast(I32))
+        load_scales(v_bytes, vals_scales, (nc.sync,) * 4)
+        nc.sync.dma_start(base_sb[:], base)
 
         def quantise(name, grouped, tag):
             codes = sb.tile([P, P], U32, name=name + "_codes", align_bytes=64)
@@ -90,91 +91,85 @@ def tile_attend_gpdirect_dampened_kernel(tc, query, keys_words, keys_scales, dam
 
         lists = [offsets[:, 0:16], offsets[:, 16:32]]
 
+        by_rs = col("by_rs", 5)
+        rs_times = col("rs_times", 10)
+        for j, value in ((1, -1.0), (2, float(HALF))):
+            nc.vector.memset(by_rs[:, j : j + 1], value)
+        for j, value in ((7, 0.5), (8, -float(HALF // 2)), (9, -1.0)):
+            nc.vector.memset(rs_times[:, j : j + 1], value)
+        nc.scalar.activation(by_rs[:, 4:5], by_rs[:, 1:2], ACT.Copy, scale=-0.5 * ROOT_K)
+        nc.scalar.activation(by_rs[:, 0:1], damp_sb[:], ACT.Copy, scale=float(SLOTS))
+        nc.scalar.activation(by_rs[:, 3:4], damp_sb[:], ACT.Copy, scale=SLOTS * ROOT_K)
+
         q_bf = sb.tile([P, P, PACK], BF16, name="q_bf", align_bytes=64)
         nc.scalar.activation(q_bf[:], q_raw[:].rearrange("p j q -> p q j"), ACT.Copy)
-        g_bf = sb.tile([P, P, PACK], BF16, name="g_bf", align_bytes=64)
-        nc.scalar.activation(g_bf[:], g_raw[:].rearrange("p j q -> p q j"), ACT.Copy)
-        base_sb = sb.tile([P, SLOTS], F32, name="base_sb", tag="stage", align_bytes=64)
-        nc.sync.dma_start(base_sb[:], base)
+        inv_damp = col("inv_damp")
+        nc.vector.reciprocal(inv_damp[:], damp_sb[:])
+        nc.scalar.activation(rs_times[:, 5:6], inv_damp[:], ACT.Copy, scale=-0.5 / SLOTS)
+        nc.scalar.activation(rs_times[:, 6:7], inv_damp[:], ACT.Copy, scale=0.25, bias=-0.25)
+        nidlh = rs_times[:, 5:6]
 
+        kb = sb.tile([P, SLOTS], U8, name="kb", tag="kb", align_bytes=64)
+        gather(kb[:], k_bytes, offsets[:])
+        q_mx = quantise("q", q_bf, "k_bytes")
         kw = sb.tile([P, SLOTS], U16, name="kw", align_bytes=64)
-        gather(kw[:], k_words, offsets[:])
-        q_mx = quantise("q", q_bf, "q_scales")
         a = []
         for i, cols in enumerate(HALVES):
-            kb = sb.tile([P, HALF], U8, name=f"kb{i}", tag=f"kb{i}", align_bytes=64)
-            gather(kb[:], k_bytes, lists[i])
-            a.append(product(f"a{i}", q_mx, kw[:, cols], kb[:]))
+            gather(kw[:, cols], k_words, lists[i])
+            a.append(product(f"a{i}", q_mx, kw[:, cols], kb[:, cols]))
 
+        g_bf = sb.tile([P, P, PACK], BF16, name="g_bf", align_bytes=64)
+        nc.scalar.activation(g_bf[:], g_raw[:].rearrange("p j q -> p q j"), ACT.Copy)
+
+        neg_a = sb.tile([P, SLOTS], F32, name="neg_a", tag="neg_a", align_bytes=64)
         nm0 = col("nm0")
-        nc.vector.tensor_reduce(nm0[:], a[0][:], mybir.AxisListType.X, ALU.max, negate=True)
         nm = col("nm")
-        neg_a1 = wide("neg_a1", HALF)
-        nc.vector.tensor_scalar(neg_a1[:], a[1][:], -1.0, nm0[:], ALU.mult, ALU.min, accum_out=nm[:])
-        p = wide("p")
-        p0 = wide("p0", HALF)
-        s0 = col("s0")
-        s1 = col("s1")
-        nc.scalar.activation(p0[:], a[0][:], ACT.Exp, bias=nm0[:], scale=1.0, accum_out=s0[:])
-        nc.scalar.activation(p[:, HALVES[1]], neg_a1[:], ACT.Exp, bias=nm[:], scale=-1.0, accum_out=s1[:])
-        f0 = col("f0")
-        nc.scalar.activation(f0[:], nm0[:], ACT.Exp, bias=nm[:], scale=-1.0)
-
-        und = col("und", 2)
-        mul2(und[:, 1:2], damp_sb[:], float(SLOTS), 1.0)
-        vw = sb.tile([P, SLOTS], U16, name="vw", align_bytes=64)
-        gather(vw[:], v_words, offsets[:])
+        nc.vector.tensor_scalar(neg_a[:, HALVES[0]], a[0][:], -1.0, None, ALU.mult, ALU.min, accum_out=nm0[:])
+        nc.vector.tensor_scalar(neg_a[:, HALVES[1]], a[1][:], -1.0, nm0[:], ALU.mult, ALU.min, accum_out=nm[:])
+        p = sb.tile([P, SLOTS], F32, name="p", tag="g_raw", align_bytes=64)
         s = col("s")
-        nc.vector.tensor_scalar(s[:], s0[:], f0[:], s1[:], ALU.mult, ALU.add)
-        nc.vector.tensor_scalar(p[:, HALVES[0]], p0[:], f0[:], None, ALU.mult)
-        rs = col("rs")
-        nc.vector.reciprocal(rs[:], s[:])
-        g_mx = quantise("g", g_bf, "kb1")
-        kappa = col("kappa")
-        nc.vector.tensor_scalar(kappa[:], rs[:], damp_sb[:], float(SLOTS), ALU.mult, ALU.mult)
-        vb = sb.tile([P, SLOTS], U8, name="vb", tag="early", align_bytes=64)
+        nc.scalar.activation(p[:], neg_a[:], ACT.Exp, bias=nm[:], scale=-1.0, accum_out=s[:])
+
+        vw = sb.tile([P, SLOTS], U16, name="vw", tag="kb", align_bytes=64)
+        gather(vw[:], v_words, offsets[:])
+        rs_tile = col("rs")
+        nc.vector.reciprocal(rs_tile[:], s[:])
+        rs = rs_tile[:]
+        g_mx = quantise("g", g_bf, "neg_a")
+        nc.vector.tensor_scalar(rs_times[:, 0:5], by_rs[:], rs, None, ALU.mult)
+        kappa, nrs, rsnh = (rs_times[:, j : j + 1] for j in range(3))
         c = []
         for i, cols in enumerate(HALVES):
-            gather(vb[:, cols], v_bytes, lists[i])
-            c.append(product(f"c{i}", g_mx, vw[:, cols], vb[:, cols]))
+            vb = sb.tile([P, HALF], U8, name=f"vb{i}", tag=f"vb{i}", align_bytes=64)
+            gather(vb[:], v_bytes, lists[i])
+            c.append(product(f"c{i}", g_mx, vw[:, cols], vb[:]))
 
-        u = wide("u")
-        nc.scalar.activation(u[:], p[:], ACT.Ln, bias=1.0, scale=kappa[:], accum_out=und[:, 0:1])
+        u = sb.tile([P, SLOTS], F32, name="u", tag="u", align_bytes=64)
+        usum = col("usum")
+        nc.scalar.activation(u[:], p[:], ACT.Ln, bias=1.0, scale=kappa, accum_out=usum[:])
         qq = wide("qq")
         qs = col("qs", 2)
         for i, cols in enumerate(HALVES):
             nc.scalar.activation(qq[:, cols], u[:, cols], ACT.Exp, scale=-1.0, accum_out=qs[:, i : i + 1])
 
-        nrs = col("nrs")
-        mul2(nrs[:], rs[:], -1.0, 1.0)
-        nrs2 = col("nrs2")
-        mul2(nrs2[:], rs[:], rs[:], -1.0)
-        rsnh = col("rsnh")
-        mul2(rsnh[:], rs[:], float(HALF), 1.0)
-        ct = col("ct", 2)
-        mul2(ct[:, 1:2], rs[:], 0.5, 1.0)
-
-        r2 = col("r2", 2)
-        nc.vector.reciprocal(r2[:], und[:])
-        ru = r2[:, 0:1]
-        idl = r2[:, 1:2]
-        ks = col("ks")
-        mul2(ks[:], kappa[:], ru, ROOT_K)
-        rsigh = col("rsigh")
-        mul2(rsigh[:], rs[:], ru, 0.5 * ROOT_K)
-        nr2 = col("nr2", 2)
-        mul2(nr2[:], r2[:], -1.0, 1.0)
-        nru = nr2[:, 0:1]
-        nidl = nr2[:, 1:2]
-        mul2(ct[:, 0:1], ru, -0.5, 1.0)
-        ruidlh = col("ruidlh")
-        mul2(ruidlh[:], ru, idl, 0.5)
-
-        uc_terms = wide("uc_terms")
         uc = col("uc", 2)
-        for i, cols in enumerate(HALVES):
-            nc.vector.scalar_tensor_tensor(uc_terms[:, cols], c[i][:], 1.0, u[:, cols], ALU.mult, ALU.mult, accum_out=uc[:, i : i + 1])
+        p2 = col("p2", 2)
         f = col("f")
+
+        def row_sum(tag, in0, scalar, in1, total):
+            terms = sb.tile([P, HALF], F32, name="terms", tag=tag, align_bytes=64)
+            nc.vector.scalar_tensor_tensor(terms[:], in0, scalar, in1, ALU.mult, ALU.mult, accum_out=total)
+
+        row_sum("vb0", p[:, HALVES[0]], nrs, p[:, HALVES[0]], p2[:, 0:1])
+        row_sum("uc0_terms", c[0][:], 1.0, u[:, HALVES[0]], uc[:, 0:1])
+        ru_tile = sb.tile([P, 1], F32, name="ru", tag="vb1", align_bytes=64)
+        nc.vector.reciprocal(ru_tile[:], usum[:])
+        ru = ru_tile[:]
+        row_sum("uc1_terms", c[1][:], 1.0, u[:, HALVES[1]], uc[:, 1:2])
+        ru_times = col("ru_times", 7)
+        nc.vector.tensor_scalar(ru_times[:], rs_times[:, 3:10], ru, None, ALU.mult)
+        ks, rsigh, c2_scale, c2_bias, ruh, t_bias, nru = (ru_times[:, j : j + 1] for j in range(7))
+        row_sum("kb", p[:, HALVES[1]], nrs, p[:, HALVES[1]], p2[:, 1:2])
         nc.vector.tensor_scalar(f[:], uc[:, 0:1], uc[:, 1:2], ru, ALU.add, ALU.mult)
         dp = wide("dp")
         pd = col("pd", 2)
@@ -189,35 +184,32 @@ def tile_attend_gpdirect_dampened_kernel(tc, query, keys_words, keys_scales, dam
                                                accum_out=sums[:, i : i + 1] if with_sum else None)
             return r, sums
 
-        h, hs = halves("h", dp, ks[:], qq, ALU.mult, ALU.mult, True)
+        h, hs = halves("h", dp, ks, qq, ALU.mult, ALU.mult, True)
         nht, nth = halves("nht", qq, 1.0, h, ALU.subtract, ALU.mult, True)
 
-        p_sq = wide("p_sq")
-        p2 = col("p2")
-        nc.scalar.activation(p_sq[:], p[:], ACT.Square, accum_out=p2[:])
-        na = fma_sum("na", hs, nrs[:], 0.0)
-        e = fma("e", p2[:], nrs2[:], nidl)
-        tt = fma_sum("tt", qs, -1.0, float(HALF))
-        b0h = fma_sum("b0h", pd, rsigh[:], 0.0)
-        cth = fma("cth", tt[:], ruidlh[:], ct[:, 0:1])
+        na = fma_sum("na", hs, nrs, 0.0)
+        cth = fma_sum("cth", qs, c2_scale, c2_bias)
+        t_nruh = fma_sum("t_nruh", qs, ruh, t_bias)
+        e = fma_sum("e", p2, rs, nidlh)
+        b0h = fma_sum("b0h", pd, rsigh, 0.0)
         beta = fma_sum("beta", hs, e[:], b0h[:])
-        tv = fma("tv", ct[:], tt[:], 0.0)
         y1h = fma_sum("y1h", hs, cth[:], 0.0)
-        y2h = fma("y2h", beta[:], tv[:, 0:1], y1h[:])
+        y2h = fma("y2h", beta[:], t_nruh[:], y1h[:])
         aa = fma_sum("aa", nth, nru, y2h[:])
 
         g = halves("g", p, na[:], h, ALU.mult, ALU.add, False)[0]
         g_sq = wide("g_sq")
         bs = col("bs")
         nc.scalar.activation(g_sq[:], g[:], ACT.Square, accum_out=bs[:])
-        ab = fma("ab", aa[:], beta[:], 0.0)
         b = fma("b", bs[:], ru, 0.0)
-        e4 = fma("e4", ab[:], rsnh[:], 0.0)
+        ab = fma("ab", aa[:], beta[:], 0.0)
         cb = fma("cb", bs[:], ru, ab[:])
-        e3h = fma("e3h", b[:], tv[:, 1:2], e4[:])
+        e4 = fma("e4", ab[:], rsnh, 0.0)
+        t_rursh = fma("t_rursh", t_nruh[:], nrs, 0.0)
+        e3h = fma("e3h", bs[:], t_rursh[:], e4[:])
         m = halves("m", g, aa[:], nht, ALU.subtract, ALU.add, False)[0]
         x, xs = halves("x", g, beta[:], m, ALU.subtract, ALU.mult, True)
-        ng = fma_sum("ng", xs, nrs[:], e3h[:])
+        ng = fma_sum("ng", xs, nrs, e3h[:])
         r = halves("r", qq, b[:], base_sb, ALU.mult, ALU.add, False)[0]
         z = halves("z", x, cb[:], r, ALU.subtract, ALU.add, False)[0]
         y = halves("y", p, ng[:], z, ALU.mult, ALU.add, False)[0]

@@ -50,7 +50,7 @@ def tile_attend_gpdirect_dampened_kernel(tc, query, keys_words, keys_scales, dam
         offsets = sb.tile([P, SLOTS // 16], U16, name="offsets")
         k_words = sb.tile([P, TOKENS], U16, name="k_words", align_bytes=64)
         v_words = sb.tile([P, TOKENS], U16, name="v_words", align_bytes=64)
-        k_bytes = sb.tile([P, TOKENS], U8, name="k_bytes", tag="k_bytes", align_bytes=64)
+        k_bytes = sb.tile([P, TOKENS], U8, name="k_bytes", align_bytes=64)
         v_bytes = sb.tile([P, TOKENS], U8, name="v_bytes", align_bytes=64)
         q_raw = sb.tile([P, PACK, P], F32, name="q_raw", tag="q_raw", align_bytes=64)
         g_raw = sb.tile([P, PACK, P], F32, name="g_raw", tag="g_raw", align_bytes=64)
@@ -60,18 +60,18 @@ def tile_attend_gpdirect_dampened_kernel(tc, query, keys_words, keys_scales, dam
         nc.vector.memset(k_bytes[:].bitcast(I32), 0)
         nc.vector.memset(v_bytes[:].bitcast(I32), 0)
 
-        def load_scales(plane, rows, queues):
-            for quad, queue in enumerate(queues):
-                queue.dma_start(plane[32 * quad : 32 * quad + 4, :].bitcast(I32), rows[0, 4 * quad : 4 * quad + 4, :].bitcast(I32))
+        def load_scales(plane, rows):
+            for quad in range(4):
+                nc.sync.dma_start(plane[32 * quad : 32 * quad + 4, :].bitcast(I32), rows[0, 4 * quad : 4 * quad + 4, :].bitcast(I32))
 
-        nc.sync.dma_start(q_raw[:], query.rearrange("(p j) q -> p j q", j=PACK))
-        nc.scalar.dma_start(damp_sb[:], damp)
-        nc.sync.dma_start(offsets[:], offs)
-        load_scales(k_bytes, keys_scales, (nc.sync,) * 4)
         nc.sync.dma_start(k_words[:].bitcast(I32), keys_words[0].bitcast(I32))
+        nc.sync.dma_start(offsets[:], offs)
+        nc.gpsimd.dma_start(damp_sb[:], damp)
+        load_scales(k_bytes, keys_scales)
+        nc.sync.dma_start(q_raw[:], query.rearrange("(p j) q -> p j q", j=PACK))
         nc.sync.dma_start(g_raw[:], gout.rearrange("(p j) q -> p j q", j=PACK))
         nc.sync.dma_start(v_words[:].bitcast(I32), vals_words[0].bitcast(I32))
-        load_scales(v_bytes, vals_scales, (nc.sync,) * 4)
+        load_scales(v_bytes, vals_scales)
         nc.sync.dma_start(base_sb[:], base)
 
         def quantise(name, grouped, tag):
@@ -97,27 +97,27 @@ def tile_attend_gpdirect_dampened_kernel(tc, query, keys_words, keys_scales, dam
             nc.vector.memset(by_rs[:, j : j + 1], value)
         for j, value in ((7, 0.5), (8, -float(HALF // 2)), (9, -1.0)):
             nc.vector.memset(rs_times[:, j : j + 1], value)
+        by_idl = col("by_idl", 4)
+        for j, value in enumerate((-0.5, float(HALF // 2), 0.0, -0.25)):
+            nc.vector.memset(by_idl[:, j : j + 1], value)
         nc.scalar.activation(by_rs[:, 4:5], by_rs[:, 1:2], ACT.Copy, scale=-0.5 * ROOT_K)
-        nc.scalar.activation(by_rs[:, 0:1], damp_sb[:], ACT.Copy, scale=float(SLOTS))
-        nc.scalar.activation(by_rs[:, 3:4], damp_sb[:], ACT.Copy, scale=SLOTS * ROOT_K)
 
-        q_bf = sb.tile([P, P, PACK], BF16, name="q_bf", align_bytes=64)
+        q_bf = sb.tile([P, P, PACK], BF16, name="q_bf", tag="q_bf", align_bytes=64)
         nc.scalar.activation(q_bf[:], q_raw[:].rearrange("p j q -> p q j"), ACT.Copy)
-        inv_damp = col("inv_damp")
-        nc.vector.reciprocal(inv_damp[:], damp_sb[:])
-        nc.scalar.activation(rs_times[:, 5:6], inv_damp[:], ACT.Copy, scale=-0.5 / SLOTS)
-        nc.scalar.activation(rs_times[:, 6:7], inv_damp[:], ACT.Copy, scale=0.25, bias=-0.25)
-        nidlh = rs_times[:, 5:6]
 
-        kb = sb.tile([P, SLOTS], U8, name="kb", tag="kb", align_bytes=64)
-        gather(kb[:], k_bytes, offsets[:])
-        q_mx = quantise("q", q_bf, "k_bytes")
-        kw = sb.tile([P, SLOTS], U16, name="kw", align_bytes=64)
-        a = []
-        for i, cols in enumerate(HALVES):
-            gather(kw[:, cols], k_words, lists[i])
-            a.append(product(f"a{i}", q_mx, kw[:, cols], kb[:, cols]))
+        kw = sb.tile([P, SLOTS], U16, name="kw", tag="picked_words", align_bytes=64)
+        gather(kw[:], k_words, offsets[:])
+        kb0 = sb.tile([P, HALF], U8, name="kb0", align_bytes=64)
+        gather(kb0[:], k_bytes, lists[0])
+        q_mx = quantise("q", q_bf, "q_scales")
+        kb1 = sb.tile([P, HALF], U8, name="kb1", tag="q_raw", align_bytes=64)
+        gather(kb1[:], k_bytes, lists[1])
+        a = [product(f"a{i}", q_mx, kw[:, HALVES[i]], kb[:]) for i, kb in enumerate((kb0, kb1))]
 
+        s_nd = sb.tile([P, 2], F32, name="s_nd", tag="q_bf", align_bytes=64)
+        nc.scalar.activation(s_nd[:, 1:2], damp_sb[:], ACT.Copy, scale=float(SLOTS))
+        nc.scalar.copy(by_rs[:, 0:1], s_nd[:, 1:2])
+        nc.scalar.activation(by_rs[:, 3:4], s_nd[:, 1:2], ACT.Copy, scale=ROOT_K)
         g_bf = sb.tile([P, P, PACK], BF16, name="g_bf", align_bytes=64)
         nc.scalar.activation(g_bf[:], g_raw[:].rearrange("p j q -> p q j"), ACT.Copy)
 
@@ -127,16 +127,17 @@ def tile_attend_gpdirect_dampened_kernel(tc, query, keys_words, keys_scales, dam
         nc.vector.tensor_scalar(neg_a[:, HALVES[0]], a[0][:], -1.0, None, ALU.mult, ALU.min, accum_out=nm0[:])
         nc.vector.tensor_scalar(neg_a[:, HALVES[1]], a[1][:], -1.0, nm0[:], ALU.mult, ALU.min, accum_out=nm[:])
         p = sb.tile([P, SLOTS], F32, name="p", tag="g_raw", align_bytes=64)
-        s = col("s")
-        nc.scalar.activation(p[:], neg_a[:], ACT.Exp, bias=nm[:], scale=-1.0, accum_out=s[:])
+        nc.scalar.activation(p[:], neg_a[:], ACT.Exp, bias=nm[:], scale=-1.0, accum_out=s_nd[:, 0:1])
 
-        vw = sb.tile([P, SLOTS], U16, name="vw", tag="kb", align_bytes=64)
+        vw = sb.tile([P, SLOTS], U16, name="vw", tag="picked_words", align_bytes=64)
         gather(vw[:], v_words, offsets[:])
-        rs_tile = col("rs")
-        nc.vector.reciprocal(rs_tile[:], s[:])
-        rs = rs_tile[:]
+        r1 = col("r1", 2)
+        nc.vector.reciprocal(r1[:], s_nd[:])
+        rs = r1[:, 0:1]
         g_mx = quantise("g", g_bf, "neg_a")
         nc.vector.tensor_scalar(rs_times[:, 0:5], by_rs[:], rs, None, ALU.mult)
+        nc.vector.scalar_tensor_tensor(rs_times[:, 5:7], by_idl[:, 0:2], r1[:, 1:2], by_idl[:, 2:4], ALU.mult, ALU.add)
+        nidlh = rs_times[:, 5:6]
         kappa, nrs, rsnh = (rs_times[:, j : j + 1] for j in range(3))
         c = []
         for i, cols in enumerate(HALVES):
@@ -169,7 +170,7 @@ def tile_attend_gpdirect_dampened_kernel(tc, query, keys_words, keys_scales, dam
         ru_times = col("ru_times", 7)
         nc.vector.tensor_scalar(ru_times[:], rs_times[:, 3:10], ru, None, ALU.mult)
         ks, rsigh, c2_scale, c2_bias, ruh, t_bias, nru = (ru_times[:, j : j + 1] for j in range(7))
-        row_sum("kb", p[:, HALVES[1]], nrs, p[:, HALVES[1]], p2[:, 1:2])
+        row_sum("picked_words", p[:, HALVES[1]], nrs, p[:, HALVES[1]], p2[:, 1:2])
         nc.vector.tensor_scalar(f[:], uc[:, 0:1], uc[:, 1:2], ru, ALU.add, ALU.mult)
         dp = wide("dp")
         pd = col("pd", 2)

import math
from contextlib import ExitStack

import concourse.mybir as mybir

F32 = mybir.dt.float32
BF16 = mybir.dt.bfloat16
I32 = mybir.dt.int32
U32 = mybir.dt.uint32
U16 = mybir.dt.uint16
U8 = mybir.dt.uint8
FP8X4 = mybir.dt.float8_e4m3fn_x4
FP4X4 = mybir.dt.float4_e2m1fn_x4
ALU = mybir.AluOpType
ACT = mybir.ActivationFunctionType

P = 128
PACK = 4
TOKENS = 2048
SLOTS = 512
HALF = SLOTS // 2
HALVES = [slice(0, HALF), slice(HALF, SLOTS)]
ROOT_K = math.sqrt(2.0 * SLOTS * SLOTS)
FLOPS = 2 * 2 * 512 * 128 * 512


def tile_attend_gpdirect_dampened_kernel(tc, query, keys_words, keys_scales, damp, gout, vals_words, vals_scales, base, offs, out):
    nc = tc.nc
    with ExitStack() as ctx:
        sb = ctx.enter_context(tc.tile_pool(name="sb", bufs=1))
        ps = ctx.enter_context(tc.psum_pool(name="ps", bufs=1))

        def wide(name, width=SLOTS):
            return sb.tile([P, width], F32, name=name, align_bytes=64)

        def col(name, width=1):
            return sb.tile([P, width], F32, name=name)

        def fma(name, x, scale, bias):
            r = col(name, x.shape[1])
            nc.scalar.activation(r[:], x, ACT.Identity, bias=bias, scale=scale)
            return r

        def fma_sum(name, x, scale, bias):
            terms = col(name + "_terms", 2)
            r = col(name)
            nc.scalar.activation(terms[:], x[:], ACT.Identity, bias=bias, scale=scale, accum_out=r[:])
            return r

        offsets = sb.tile([P, SLOTS // 16], U16, name="offsets")
        k_words = sb.tile([P, TOKENS], U16, name="k_words", align_bytes=64)
        v_words = sb.tile([P, TOKENS], U16, name="v_words", align_bytes=64)
        k_bytes = sb.tile([P, TOKENS], U8, name="k_bytes", align_bytes=64)
        v_bytes = sb.tile([P, TOKENS], U8, name="v_bytes", align_bytes=64)
        q_raw = sb.tile([P, PACK, P], F32, name="q_raw", tag="q_raw", align_bytes=64)
        g_raw = sb.tile([P, PACK, P], F32, name="g_raw", tag="g_raw", align_bytes=64)
        damp_sb = col("damp_sb")
        base_sb = wide("base_sb")

        nc.vector.memset(k_bytes[:].bitcast(I32), 0)
        nc.vector.memset(v_bytes[:].bitcast(I32), 0)

        def load_scales(plane, rows):
            for quad in range(4):
                nc.sync.dma_start(plane[32 * quad : 32 * quad + 4, :].bitcast(I32), rows[0, 4 * quad : 4 * quad + 4, :].bitcast(I32))

        nc.sync.dma_start(k_words[:].bitcast(I32), keys_words[0].bitcast(I32))
        nc.sync.dma_start(offsets[:], offs)
        nc.gpsimd.dma_start(damp_sb[:], damp)
        load_scales(k_bytes, keys_scales)
        nc.sync.dma_start(q_raw[:], query.rearrange("(p j) q -> p j q", j=PACK))
        nc.sync.dma_start(g_raw[:], gout.rearrange("(p j) q -> p j q", j=PACK))
        nc.sync.dma_start(v_words[:].bitcast(I32), vals_words[0].bitcast(I32))
        load_scales(v_bytes, vals_scales)
        nc.sync.dma_start(base_sb[:], base)

        def quantise(name, grouped, tag):
            codes = sb.tile([P, P], U32, name=name + "_codes", align_bytes=64)
            scales = sb.tile([P, P], U8, name=name + "_scales", tag=tag, align_bytes=64)
            nc.vector.quantize_mx(out=codes[:].bitcast(FP8X4), scales=scales[:], in_=grouped[:].rearrange("p q j -> p (q j)"))
            return codes, scales

        def gather(picked, window, lst):
            nc.vector.tensor_copy(picked, window[:].indirect(lst))

        def product(name, stationary, words, scale_bytes):
            bank = ps.tile([P, HALF], F32, name=name)
            nc.tensor.matmul_mx(out=bank[:], lhsT=stationary[0][:].bitcast(FP8X4), lhsT_scale=stationary[1][:],
                                rhs=words.bitcast(FP4X4), rhs_scale=scale_bytes, start=True, stop=True)
            return bank

        lists = [offsets[:, 0:16], offsets[:, 16:32]]

        by_rs = col("by_rs", 5)
        rs_times = col("rs_times", 10)
        for j, value in ((1, -1.0), (2, float(HALF))):
            nc.vector.memset(by_rs[:, j : j + 1], value)
        for j, value in ((7, 0.5), (8, -float(HALF // 2)), (9, -1.0)):
            nc.vector.memset(rs_times[:, j : j + 1], value)
        by_idl = col("by_idl", 4)
        for j, value in enumerate((-0.5, float(HALF // 2), 0.0, -0.25)):
            nc.vector.memset(by_idl[:, j : j + 1], value)
        nc.scalar.activation(by_rs[:, 4:5], by_rs[:, 1:2], ACT.Copy, scale=-0.5 * ROOT_K)

        q_bf = sb.tile([P, P, PACK], BF16, name="q_bf", tag="q_bf", align_bytes=64)
        nc.scalar.activation(q_bf[:], q_raw[:].rearrange("p j q -> p q j"), ACT.Copy)

        kw = sb.tile([P, SLOTS], U16, name="kw", tag="picked_words", align_bytes=64)
        gather(kw[:], k_words, offsets[:])
        kb0 = sb.tile([P, HALF], U8, name="kb0", align_bytes=64)
        gather(kb0[:], k_bytes, lists[0])
        q_mx = quantise("q", q_bf, "q_scales")
        kb1 = sb.tile([P, HALF], U8, name="kb1", tag="q_raw", align_bytes=64)
        gather(kb1[:], k_bytes, lists[1])
        a = [product(f"a{i}", q_mx, kw[:, HALVES[i]], kb[:]) for i, kb in enumerate((kb0, kb1))]

        s_nd = sb.tile([P, 2], F32, name="s_nd", tag="q_bf", align_bytes=64)
        nc.scalar.activation(s_nd[:, 1:2], damp_sb[:], ACT.Copy, scale=float(SLOTS))
        nc.scalar.copy(by_rs[:, 0:1], s_nd[:, 1:2])
        nc.scalar.activation(by_rs[:, 3:4], s_nd[:, 1:2], ACT.Copy, scale=ROOT_K)
        g_bf = sb.tile([P, P, PACK], BF16, name="g_bf", align_bytes=64)
        nc.scalar.activation(g_bf[:], g_raw[:].rearrange("p j q -> p q j"), ACT.Copy)

        neg_a = sb.tile([P, SLOTS], F32, name="neg_a", tag="neg_a", align_bytes=64)
        nm0 = col("nm0")
        nm = col("nm")
        nc.vector.tensor_scalar(neg_a[:, HALVES[0]], a[0][:], -1.0, None, ALU.mult, ALU.min, accum_out=nm0[:])
        nc.vector.tensor_scalar(neg_a[:, HALVES[1]], a[1][:], -1.0, nm0[:], ALU.mult, ALU.min, accum_out=nm[:])
        p = sb.tile([P, SLOTS], F32, name="p", tag="g_raw", align_bytes=64)
        nc.scalar.activation(p[:], neg_a[:], ACT.Exp, bias=nm[:], scale=-1.0, accum_out=s_nd[:, 0:1])

        vw = sb.tile([P, SLOTS], U16, name="vw", tag="picked_words", align_bytes=64)
        gather(vw[:], v_words, offsets[:])
        r1 = col("r1", 2)
        nc.vector.reciprocal(r1[:], s_nd[:])
        rs = r1[:, 0:1]
        g_mx = quantise("g", g_bf, "neg_a")
        nc.vector.tensor_scalar(rs_times[:, 0:5], by_rs[:], rs, None, ALU.mult)
        nc.vector.scalar_tensor_tensor(rs_times[:, 5:7], by_idl[:, 0:2], r1[:, 1:2], by_idl[:, 2:4], ALU.mult, ALU.add)
        nidlh = rs_times[:, 5:6]
        kappa, nrs, rsnh = (rs_times[:, j : j + 1] for j in range(3))
        c = []
        for i, cols in enumerate(HALVES):
            vb = sb.tile([P, HALF], U8, name=f"vb{i}", tag=f"vb{i}", align_bytes=64)
            gather(vb[:], v_bytes, lists[i])
            c.append(product(f"c{i}", g_mx, vw[:, cols], vb[:]))

        u = sb.tile([P, SLOTS], F32, name="u", tag="u", align_bytes=64)
        usum = col("usum")
        nc.scalar.activation(u[:], p[:], ACT.Ln, bias=1.0, scale=kappa, accum_out=usum[:])
        qq = wide("qq")
        qs = col("qs", 2)
        for i, cols in enumerate(HALVES):
            nc.scalar.activation(qq[:, cols], u[:, cols], ACT.Exp, scale=-1.0, accum_out=qs[:, i : i + 1])

        uc = col("uc", 2)
        p2 = col("p2", 2)
        f = col("f")

        def row_sum(tag, in0, scalar, in1, total):
            terms = sb.tile([P, HALF], F32, name="terms", tag=tag, align_bytes=64)
            nc.vector.scalar_tensor_tensor(terms[:], in0, scalar, in1, ALU.mult, ALU.mult, accum_out=total)

        row_sum("vb0", p[:, HALVES[0]], nrs, p[:, HALVES[0]], p2[:, 0:1])
        row_sum("uc0_terms", c[0][:], 1.0, u[:, HALVES[0]], uc[:, 0:1])
        ru_tile = sb.tile([P, 1], F32, name="ru", tag="vb1", align_bytes=64)
        nc.vector.reciprocal(ru_tile[:], usum[:])
        ru = ru_tile[:]
        row_sum("uc1_terms", c[1][:], 1.0, u[:, HALVES[1]], uc[:, 1:2])
        ru_times = col("ru_times", 7)
        nc.vector.tensor_scalar(ru_times[:], rs_times[:, 3:10], ru, None, ALU.mult)
        ks, rsigh, c2_scale, c2_bias, ruh, t_bias, nru = (ru_times[:, j : j + 1] for j in range(7))
        row_sum("picked_words", p[:, HALVES[1]], nrs, p[:, HALVES[1]], p2[:, 1:2])
        nc.vector.tensor_scalar(f[:], uc[:, 0:1], uc[:, 1:2], ru, ALU.add, ALU.mult)
        dp = wide("dp")
        pd = col("pd", 2)
        for i, cols in enumerate(HALVES):
            nc.vector.scalar_tensor_tensor(dp[:, cols], c[i][:], f[:], p[:, cols], ALU.subtract, ALU.mult, accum_out=pd[:, i : i + 1])

        def halves(name, in0, scalar, in1, op0, op1, with_sum):
            r = wide(name)
            sums = col(name + "_sums", 2) if with_sum else None
            for i, cols in enumerate(HALVES):
                nc.vector.scalar_tensor_tensor(r[:, cols], in0[:, cols], scalar, in1[:, cols], op0, op1,
                                               accum_out=sums[:, i : i + 1] if with_sum else None)
            return r, sums

        h, hs = halves("h", dp, ks, qq, ALU.mult, ALU.mult, True)
        nht, nth = halves("nht", qq, 1.0, h, ALU.subtract, ALU.mult, True)

        na = fma_sum("na", hs, nrs, 0.0)
        cth = fma_sum("cth", qs, c2_scale, c2_bias)
        t_nruh = fma_sum("t_nruh", qs, ruh, t_bias)
        e = fma_sum("e", p2, rs, nidlh)
        b0h = fma_sum("b0h", pd, rsigh, 0.0)
        beta = fma_sum("beta", hs, e[:], b0h[:])
        y1h = fma_sum("y1h", hs, cth[:], 0.0)
        y2h = fma("y2h", beta[:], t_nruh[:], y1h[:])
        aa = fma_sum("aa", nth, nru, y2h[:])

        g = halves("g", p, na[:], h, ALU.mult, ALU.add, False)[0]
        g_sq = wide("g_sq")
        bs = col("bs")
        nc.scalar.activation(g_sq[:], g[:], ACT.Square, accum_out=bs[:])
        b = fma("b", bs[:], ru, 0.0)
        ab = fma("ab", aa[:], beta[:], 0.0)
        cb = fma("cb", bs[:], ru, ab[:])
        e4 = fma("e4", ab[:], rsnh, 0.0)
        t_rursh = fma("t_rursh", t_nruh[:], nrs, 0.0)
        e3h = fma("e3h", bs[:], t_rursh[:], e4[:])
        m = halves("m", g, aa[:], nht, ALU.subtract, ALU.add, False)[0]
        x, xs = halves("x", g, beta[:], m, ALU.subtract, ALU.mult, True)
        ng = fma_sum("ng", xs, nrs, e3h[:])
        r = halves("r", qq, b[:], base_sb, ALU.mult, ALU.add, False)[0]
        z = halves("z", x, cb[:], r, ALU.subtract, ALU.add, False)[0]
        y = halves("y", p, ng[:], z, ALU.mult, ALU.add, False)[0]
        nc.sync.dma_start(out[:, HALVES[0]], y[:, HALVES[0]])
        nc.scalar.dma_start(out[:, HALVES[1]], y[:, HALVES[1]])
